import numpy as np
import ml_dtypes

BF16 = ml_dtypes.bfloat16


def bf(x):
    return np.asarray(x, np.float32).astype(BF16)


def f32(x):
    return np.asarray(x, np.float32)


def f64(x):
    return np.asarray(x).astype(np.float64)


def striped(idx):
    return np.tile(idx.reshape(-1, 16).T, (8, 1))


S, K, M, N, V, D = 1024, 512, 256, 1024, 128, 8


def setup_inputs():
    return {"table": bf(np.random.standard_normal((K, S))), "w": bf(np.random.standard_normal((K, M)) / np.sqrt(K)), "c": f32((0.2 + 0.8 * np.random.random_sample((1, N))) / np.sqrt(D)), "b": f32(0.5 * np.random.standard_normal((M, 1))), "offs": striped(np.random.permutation(np.tile(np.arange(S), 2))[:N])}


def reference(table, w, c, b, offs):
    idx = offs[:16].T.reshape(-1)
    y = (f64(w).T @ f64(table)[:, idx]).reshape(M, V, D)
    a = f64(c).reshape(V, D)
    z = (y * a).sum(axis=2)
    return np.tanh(z + f64(b))

@@ -1,0 +1,70 @@
+import concourse.mybir as mybir
+
+P = 128
+S, K, M, N = 1024, 512, 256, 1024
+BAG = 8
+PIECE = 512
+K_BLOCKS, M_BLOCKS, PIECES = K // P, M // P, N // PIECE
+BAGS, PIECE_BAGS = N // BAG, PIECE // BAG
+PIECE_COLS = PIECE // 16
+
+FLOPS = 2 * K * M * N
+
+BF16, F32, U16 = mybir.dt.bfloat16, mybir.dt.float32, mybir.dt.uint16
+
+
+def tile_rows_wbag_tanh_rep_kernel(tc, table, w, c, b, offs, out):
+    nc = tc.nc
+    table_blocks = table.rearrange("(p k) s -> k p s", k=K_BLOCKS)
+    w_rows = w.rearrange("(p k) m -> p k m", k=K_BLOCKS)
+
+    with (
+        tc.tile_pool(name="held", bufs=1) as held,
+        tc.tile_pool(name="work", bufs=2) as work,
+        tc.psum_pool(name="psum", bufs=M_BLOCKS * PIECES) as psum,
+    ):
+        offsets = held.tile([P, N // 16], U16, name="offsets")
+        words = [held.tile([P, S], BF16, name=f"words{k}") for k in range(K_BLOCKS)]
+        w_first = held.tile([P, 1, M], BF16, name="w_first")
+        w_rest = held.tile([P, K_BLOCKS - 1, M], BF16, name="w_rest")
+        bag_weights = held.tile([P, N], F32, name="bag_weights")
+        bias = held.tile([P, M_BLOCKS], F32, name="bias")
+
+        nc.sync.dma_start(words[0][:], table_blocks[0])
+        nc.scalar.dma_start(w_first[:], w_rows[:, 0:1, :])
+        nc.sync.dma_start(offsets[:], offs)
+        nc.sync.dma_start(w_rest[:], w_rows[:, 1:, :])
+        for k in range(1, K_BLOCKS):
+            nc.sync.dma_start(words[k][:], table_blocks[k])
+        nc.sync.dma_start(bag_weights[:], c[0].partition_broadcast(P))
+        nc.sync.dma_start(bias[:], b.rearrange("(a p) o -> p (a o)", p=P))
+
+        def weight_block(k, m):
+            columns = slice(m * P, (m + 1) * P)
+            return w_first[:, 0, columns] if k == 0 else w_rest[:, k - 1, columns]
+
+        for m in range(M_BLOCKS):
+            result = work.tile([P, BAGS], F32, name="result")
+            for piece in range(PIECES):
+                picked = offsets[:, piece * PIECE_COLS : (piece + 1) * PIECE_COLS]
+                y = psum.tile([P, PIECE], F32, name="y")
+                for k in range(K_BLOCKS):
+                    nc.tensor.matmul(
+                        y[:], weight_block(k, m), words[k][:].indirect(picked),
+                        start=(k == 0), stop=(k == K_BLOCKS - 1),
+                    )
+                weighted = work.tile([P, PIECE], F32, name="weighted")
+                nc.vector.tensor_tensor(
+                    weighted[:], y[:], bag_weights[:, piece * PIECE : (piece + 1) * PIECE],
+                    mybir.AluOpType.mult,
+                )
+                z = work.tile([P, PIECE_BAGS], F32, name="z")
+                nc.vector.tensor_reduce(
+                    z[:], weighted[:].rearrange("p (v t) -> p v t", t=BAG),
+                    mybir.AxisListType.X, mybir.AluOpType.add,
+                )
+                nc.scalar.activation(
+                    result[:, piece * PIECE_BAGS : (piece + 1) * PIECE_BAGS], z[:],
+                    mybir.ActivationFunctionType.Tanh, bias=bias[:, m : m + 1],
+                )
+            nc.sync.dma_start(out[m * P : (m + 1) * P, :], result[:])

@@ -6,6 +6,7 @@ BAG = 8
 PIECE = 512
 K_BLOCKS, M_BLOCKS, PIECES = K // P, M // P, N // PIECE
 BAGS, PIECE_BAGS = N // BAG, PIECE // BAG
+HALF, HALF_BAGS = PIECE // 2, PIECE_BAGS // 2
 PIECE_COLS = PIECE // 16
 
 FLOPS = 2 * K * M * N
@@ -21,7 +22,7 @@ def tile_rows_wbag_tanh_rep_kernel(tc, table, w, c, b, offs, out):
     with (
         tc.tile_pool(name="held", bufs=1) as held,
         tc.tile_pool(name="work", bufs=2) as work,
-        tc.psum_pool(name="psum", bufs=M_BLOCKS * PIECES) as psum,
+        tc.psum_pool(name="psum", bufs=3) as psum,
     ):
         offsets = held.tile([P, N // 16], U16, name="offsets")
         words = [held.tile([P, S], BF16, name=f"words{k}") for k in range(K_BLOCKS)]
@@ -53,16 +54,19 @@ def tile_rows_wbag_tanh_rep_kernel(tc, table, w, c, b, offs, out):
                         y[:], weight_block(k, m), words[k][:].indirect(picked),
                         start=(k == 0), stop=(k == K_BLOCKS - 1),
                     )
-                weighted = work.tile([P, PIECE], F32, name="weighted")
-                nc.vector.tensor_tensor(
-                    weighted[:], y[:], bag_weights[:, piece * PIECE : (piece + 1) * PIECE],
-                    mybir.AluOpType.mult,
-                )
                 z = work.tile([P, PIECE_BAGS], F32, name="z")
-                nc.vector.tensor_reduce(
-                    z[:], weighted[:].rearrange("p (v t) -> p v t", t=BAG),
-                    mybir.AxisListType.X, mybir.AluOpType.add,
-                )
+                for half in range(2):
+                    first = piece * PIECE + half * HALF
+                    weighted = work.tile([P, HALF], F32, name="weighted")
+                    nc.vector.tensor_tensor(
+                        weighted[:], y[:, half * HALF : (half + 1) * HALF],
+                        bag_weights[:, first : first + HALF], mybir.AluOpType.mult,
+                    )
+                    nc.vector.tensor_reduce(
+                        z[:, half * HALF_BAGS : (half + 1) * HALF_BAGS],
+                        weighted[:].rearrange("p (v t) -> p v t", t=BAG),
+                        mybir.AxisListType.X, mybir.AluOpType.add,
+                    )
                 nc.scalar.activation(
                     result[:, piece * PIECE_BAGS : (piece + 1) * PIECE_BAGS], z[:],
                     mybir.ActivationFunctionType.Tanh, bias=bias[:, m : m + 1],

import concourse.mybir as mybir

P = 128
S, K, M, N = 1024, 512, 256, 1024
BAG = 8
PIECE = 512
K_BLOCKS, M_BLOCKS, PIECES = K // P, M // P, N // PIECE
BAGS, PIECE_BAGS = N // BAG, PIECE // BAG
HALF, HALF_BAGS = PIECE // 2, PIECE_BAGS // 2
PIECE_COLS = PIECE // 16

FLOPS = 2 * K * M * N

BF16, F32, U16 = mybir.dt.bfloat16, mybir.dt.float32, mybir.dt.uint16


def tile_rows_wbag_tanh_rep_kernel(tc, table, w, c, b, offs, out):
    nc = tc.nc
    table_blocks = table.rearrange("(p k) s -> k p s", k=K_BLOCKS)
    w_rows = w.rearrange("(p k) m -> p k m", k=K_BLOCKS)

    with (
        tc.tile_pool(name="held", bufs=1) as held,
        tc.tile_pool(name="work", bufs=2) as work,
        tc.psum_pool(name="psum", bufs=3) as psum,
    ):
        offsets = held.tile([P, N // 16], U16, name="offsets")
        words = [held.tile([P, S], BF16, name=f"words{k}") for k in range(K_BLOCKS)]
        w_first = held.tile([P, 1, M], BF16, name="w_first")
        w_rest = held.tile([P, K_BLOCKS - 1, M], BF16, name="w_rest")
        bag_weights = held.tile([P, N], F32, name="bag_weights")
        bias = held.tile([P, M_BLOCKS], F32, name="bias")

        nc.sync.dma_start(words[0][:], table_blocks[0])
        nc.scalar.dma_start(w_first[:], w_rows[:, 0:1, :])
        nc.sync.dma_start(offsets[:], offs)
        nc.sync.dma_start(w_rest[:], w_rows[:, 1:, :])
        for k in range(1, K_BLOCKS):
            nc.sync.dma_start(words[k][:], table_blocks[k])
        nc.sync.dma_start(bag_weights[:], c[0].partition_broadcast(P))
        nc.sync.dma_start(bias[:], b.rearrange("(a p) o -> p (a o)", p=P))

        def weight_block(k, m):
            columns = slice(m * P, (m + 1) * P)
            return w_first[:, 0, columns] if k == 0 else w_rest[:, k - 1, columns]

        for m in range(M_BLOCKS):
            result = work.tile([P, BAGS], F32, name="result")
            for piece in range(PIECES):
                picked = offsets[:, piece * PIECE_COLS : (piece + 1) * PIECE_COLS]
                y = psum.tile([P, PIECE], F32, name="y")
                for k in range(K_BLOCKS):
                    nc.tensor.matmul(
                        y[:], weight_block(k, m), words[k][:].indirect(picked),
                        start=(k == 0), stop=(k == K_BLOCKS - 1),
                    )
                z = work.tile([P, PIECE_BAGS], F32, name="z")
                for half in range(2):
                    first = piece * PIECE + half * HALF
                    weighted = work.tile([P, HALF], F32, name="weighted")
                    nc.vector.tensor_tensor(
                        weighted[:], y[:, half * HALF : (half + 1) * HALF],
                        bag_weights[:, first : first + HALF], mybir.AluOpType.mult,
                    )
                    nc.vector.tensor_reduce(
                        z[:, half * HALF_BAGS : (half + 1) * HALF_BAGS],
                        weighted[:].rearrange("p (v t) -> p v t", t=BAG),
                        mybir.AxisListType.X, mybir.AluOpType.add,
                    )
                nc.scalar.activation(
                    result[:, piece * PIECE_BAGS : (piece + 1) * PIECE_BAGS], z[:],
                    mybir.ActivationFunctionType.Tanh, bias=bias[:, m : m + 1],
                )
            nc.sync.dma_start(out[m * P : (m + 1) * P, :], result[:])
